import numpy as np, ml_dtypes
CORES = [16,32,48,64,80]
N = 5
TK = 256
WID = [64,32,64,256,64]
def setup_inputs(rng):
    return {"x": rng.standard_normal((N, 128, TK), dtype=np.float32).astype(ml_dtypes.bfloat16), "w1": (rng.standard_normal((N, 128, 128), dtype=np.float32) / 8).astype(ml_dtypes.bfloat16), "w2": (rng.standard_normal((N, 128, 128), dtype=np.float32) / 8).astype(ml_dtypes.bfloat16)}
def setup_inputs_big(rng):
    d = setup_inputs(rng)
    for k in ("x", "w1", "w2"): d[k] = (d[k].astype(np.float32) * 1024.0).astype(d[k].dtype)
    return d
def setup_inputs_small(rng):
    d = setup_inputs(rng)
    for k in ("x", "w1", "w2"): d[k] = (d[k].astype(np.float32) * (1 / 1024.0)).astype(d[k].dtype)
    return d
def setup_inputs_apart(rng):
    d = setup_inputs(rng)
    f = (10.0 ** rng.permutation(np.linspace(-1.5, 1.5, N))).astype(np.float32).reshape(N, 1, 1)
    for k in ("x", "w1", "w2"): d[k] = (d[k].astype(np.float32) * f).astype(d[k].dtype)
    return d
def whole(x, w1, w2):
    X, W1, W2 = x.astype(np.float64), w1.astype(np.float64), w2.astype(np.float64)
    y = np.zeros((N, 128, TK))
    for r in range(N):
        for j in range(N):
            y[r] += W2[j].T @ np.maximum(W1[j].T @ X[r], 0.0)
    return {"y": y.astype(ml_dtypes.bfloat16 if x.dtype != np.float64 else np.float64)}
def reference(x, w1, w2):
    o = whole(x, w1, w2)["y"].copy()
    for r in range(N):
        o[r][:, WID[r]:] = np.nan
    return {"y": o}

@@ -1,0 +1,106 @@
+from concourse.bass import DstId, RemoteDMATransfer
+from concourse.mybir import AluOpType
+
+N = 5
+D = 128
+TK = 256
+PIECE = 128
+NPIECE = TK // PIECE
+NH = 6
+SLOT = 2 * D
+
+SCRATCH = {
+    "wall": ("sbuf", [128, N * SLOT], "bfloat16"),
+    "xs": ("sbuf", [128, TK], "bfloat16"),
+    "zero": ("sbuf", [128, PIECE], "float32"),
+    "hs": ("sbuf", [128, N * TK], "bfloat16"),
+    "ys": ("sbuf", [128, TK], "bfloat16"),
+}
+for _i in range(NH):
+    SCRATCH["h%d" % _i] = ("psum", [128, 512], "float32")
+for _i in range(NPIECE):
+    SCRATCH["y%d" % _i] = ("psum", [128, 512], "float32")
+
+SEMAPHORES = (["wl", "xl", "zs", "sent", "cp", "st"]
+              + ["arr%d" % j for j in range(N)]
+              + ["m%d" % k for k in range(N * NPIECE)]
+              + ["r%d" % k for k in range(N * NPIECE)]
+              + ["a%d" % p for p in range(NPIECE)])
+
+
+def _peers(T, rank):
+    n = len(T.cores)
+    return [T.cores[(rank + s) % n] for s in range(1, n)]
+
+
+def _mask(T, topo, rank):
+    src = T.cores[rank]
+    m = None
+    for p in _peers(T, rank):
+        assert topo.may_write(src, p)
+        m = topo.mask(src, p) if m is None else (m & topo.mask(src, p))
+    return m
+
+
+def _engines(T, topo, rank):
+    return bin(_mask(T, topo, rank)).count("1")
+
+
+def rank_program(g, core, T, topo):
+    rank = T.rank_of(core)
+    if rank is None:
+        return
+    n = len(T.cores)
+    W = T.tables["WID"][rank]
+    sem = T.sem
+    base = rank * SLOT
+    own = T.wall[:, base:base + SLOT]
+
+    g.sync.dma_start(T.wall[:, base:base + D], T.w1[:, :]).then_inc(sem.wl, 16)
+    g.scalar.dma_start(T.wall[:, base + D:base + SLOT], T.w2[:, :]).then_inc(sem.wl, 16)
+    g.sync.dma_start(T.xs[:, 0:W], T.x[:, 0:W]).then_inc(sem.xl, 16)
+    g.vector.memset(T.zero[:, :], 0.0).then_inc(sem.zs, 1)
+
+    peers = _peers(T, rank)
+    ids = []
+    for p in peers:
+        rid, pid, _se = topo.addr(p)
+        ids.append(DstId(rid=rid, pnc=pid))
+    g.wait_ge(sem.wl, 32)
+    g.remote_dma_fused(
+        [RemoteDMATransfer(dst_ids=ids, dma_engine_mask=_mask(T, topo, rank), remote_sem=sem["arr%d" % rank],
+                           srcs=[own], dsts=[own for _p in peers], alu_op=0)],
+        local_sem=sem.sent)
+
+    pieces = [(a, min(a + PIECE, W)) for a in range(0, W, PIECE)]
+    g.vector.wait_ge(sem.zs, 1)
+    k = 0
+    for si in range(n):
+        s = (rank - si) % n
+        w1 = T.wall[:, s * SLOT:s * SLOT + D]
+        w2 = T.wall[:, s * SLOT + D:(s + 1) * SLOT]
+        if s == rank:
+            g.tensor.wait_ge(sem.wl, 32)
+            g.tensor.wait_ge(sem.xl, 16)
+        else:
+            g.tensor.wait_ge(sem["arr%d" % s], _engines(T, topo, s))
+        first = k
+        for (a, b) in pieces:
+            hb = T["h%d" % (k % NH)]
+            g.tensor.matmul(hb[:, 0:b - a], w1, T.xs[:, a:b], True, True).then_inc(sem["m%d" % k], 1)
+            g.vector.wait_ge(sem["m%d" % k], 1)
+            g.vector.tensor_tensor(T.hs[:, s * TK + a:s * TK + b], hb[:, 0:b - a], T.zero[:, 0:b - a],
+                                   AluOpType.max).then_inc(sem["r%d" % k], 1)
+            k += 1
+        for p, (a, b) in enumerate(pieces):
+            g.tensor.wait_ge(sem["r%d" % (first + p)], 1)
+            g.tensor.matmul(T["y%d" % p][:, 0:b - a], w2, T.hs[:, s * TK + a:s * TK + b],
+                            si == 0, si == n - 1).then_inc(sem["a%d" % p], 1)
+
+    for p, (a, b) in enumerate(pieces):
+        g.vector.wait_ge(sem["a%d" % p], n)
+        g.vector.tensor_copy(T.ys[:, a:b], T["y%d" % p][:, 0:b - a]).then_inc(sem.cp, 1)
+    g.sync.wait_ge(sem.cp, len(pieces))
+    g.sync.dma_start(T.y[:, 0:W], T.ys[:, 0:W]).then_inc(sem.st, 16)
+    g.sync.wait_ge(sem.st, 16)
+    g.wait_ge(sem.sent, _engines(T, topo, rank))

@@ -21,7 +21,9 @@ for _i in range(NH):
 for _i in range(NPIECE):
     SCRATCH["y%d" % _i] = ("psum", [128, 512], "float32")
 
-SEMAPHORES = (["wl", "xl", "zs", "sent", "cp", "st"]
+SEMAPHORES = (["l1", "l2", "xl", "zs", "sent", "cp", "st"]
+              + ["ua%d" % j for j in range(N)]
+              + ["ub%d" % j for j in range(N)]
               + ["arr%d" % j for j in range(N)]
               + ["m%d" % k for k in range(N * NPIECE)]
               + ["r%d" % k for k in range(N * NPIECE)]
@@ -46,6 +48,14 @@ def _engines(T, topo, rank):
     return bin(_mask(T, topo, rank)).count("1")
 
 
+def _ids(topo, dsts):
+    out = []
+    for p in dsts:
+        rid, pid, _se = topo.addr(p)
+        out.append(DstId(rid=rid, pnc=pid))
+    return out
+
+
 def rank_program(g, core, T, topo):
     rank = T.rank_of(core)
     if rank is None:
@@ -54,48 +64,74 @@ def rank_program(g, core, T, topo):
     W = T.tables["WID"][rank]
     sem = T.sem
     base = rank * SLOT
+    own1 = T.wall[:, base:base + D]
+    own2 = T.wall[:, base + D:base + SLOT]
     own = T.wall[:, base:base + SLOT]
 
-    g.sync.dma_start(T.wall[:, base:base + D], T.w1[:, :]).then_inc(sem.wl, 16)
-    g.scalar.dma_start(T.wall[:, base + D:base + SLOT], T.w2[:, :]).then_inc(sem.wl, 16)
-    g.sync.dma_start(T.xs[:, 0:W], T.x[:, 0:W]).then_inc(sem.xl, 16)
+    g.sync.dma_start(own1, T.w1[:, :]).then_inc(sem.l1, 16)
+    g.sync.dma_start(own2, T.w2[:, :]).then_inc(sem.l2, 16)
+    g.scalar.wait_ge(sem.l1, 16)
+    g.scalar.dma_start(T.xs[:, 0:W], T.x[:, 0:W]).then_inc(sem.xl, 16)
     g.vector.memset(T.zero[:, :], 0.0).then_inc(sem.zs, 1)
 
     peers = _peers(T, rank)
-    ids = []
-    for p in peers:
-        rid, pid, _se = topo.addr(p)
-        ids.append(DstId(rid=rid, pnc=pid))
-    g.wait_ge(sem.wl, 32)
+    whole, split = peers[:-1], peers[-1:]
+    mask = _mask(T, topo, rank)
+    g.wait_ge(sem.l1, 16)
     g.remote_dma_fused(
-        [RemoteDMATransfer(dst_ids=ids, dma_engine_mask=_mask(T, topo, rank), remote_sem=sem["arr%d" % rank],
-                           srcs=[own], dsts=[own for _p in peers], alu_op=0)],
+        [RemoteDMATransfer(dst_ids=_ids(topo, split), dma_engine_mask=mask, remote_sem=sem["ua%d" % rank],
+                           srcs=[own1], dsts=[own1 for _p in split], alu_op=0)],
+        local_sem=sem.sent)
+    g.wait_ge(sem.l2, 16)
+    g.remote_dma_fused(
+        [RemoteDMATransfer(dst_ids=_ids(topo, whole), dma_engine_mask=mask, remote_sem=sem["arr%d" % rank],
+                           srcs=[own], dsts=[own for _p in whole], alu_op=0)],
+        local_sem=sem.sent)
+    g.remote_dma_fused(
+        [RemoteDMATransfer(dst_ids=_ids(topo, split), dma_engine_mask=mask, remote_sem=sem["ub%d" % rank],
+                           srcs=[own2], dsts=[own2 for _p in split], alu_op=0)],
         local_sem=sem.sent)
 
     pieces = [(a, min(a + PIECE, W)) for a in range(0, W, PIECE)]
-    g.vector.wait_ge(sem.zs, 1)
-    k = 0
-    for si in range(n):
-        s = (rank - si) % n
-        w1 = T.wall[:, s * SLOT:s * SLOT + D]
-        w2 = T.wall[:, s * SLOT + D:(s + 1) * SLOT]
-        if s == rank:
-            g.tensor.wait_ge(sem.wl, 32)
-            g.tensor.wait_ge(sem.xl, 16)
-        else:
-            g.tensor.wait_ge(sem["arr%d" % s], _engines(T, topo, s))
-        first = k
+    order = [(rank - si) % n for si in range(n)]
+    late = order[-1]
+    kk = [0]
+
+    def layer1(s):
+        first = kk[0]
         for (a, b) in pieces:
+            k = kk[0]
+            if k >= NH:
+                g.tensor.wait_ge(sem["r%d" % (k - NH)], 1)
             hb = T["h%d" % (k % NH)]
-            g.tensor.matmul(hb[:, 0:b - a], w1, T.xs[:, a:b], True, True).then_inc(sem["m%d" % k], 1)
+            g.tensor.matmul(hb[:, 0:b - a], T.wall[:, s * SLOT:s * SLOT + D], T.xs[:, a:b],
+                            True, True).then_inc(sem["m%d" % k], 1)
             g.vector.wait_ge(sem["m%d" % k], 1)
             g.vector.tensor_tensor(T.hs[:, s * TK + a:s * TK + b], hb[:, 0:b - a], T.zero[:, 0:b - a],
                                    AluOpType.max).then_inc(sem["r%d" % k], 1)
-            k += 1
+            kk[0] += 1
+        return first
+
+    def layer2(s, first, start, stop):
         for p, (a, b) in enumerate(pieces):
             g.tensor.wait_ge(sem["r%d" % (first + p)], 1)
-            g.tensor.matmul(T["y%d" % p][:, 0:b - a], w2, T.hs[:, s * TK + a:s * TK + b],
-                            si == 0, si == n - 1).then_inc(sem["a%d" % p], 1)
+            g.tensor.matmul(T["y%d" % p][:, 0:b - a], T.wall[:, s * SLOT + D:(s + 1) * SLOT],
+                            T.hs[:, s * TK + a:s * TK + b], start, stop).then_inc(sem["a%d" % p], 1)
+
+    g.vector.wait_ge(sem.zs, 1)
+    g.tensor.wait_ge(sem.l1, 16)
+    g.tensor.wait_ge(sem.xl, 16)
+    f_own = layer1(rank)
+    g.tensor.wait_ge(sem.l2, 16)
+    layer2(rank, f_own, True, False)
+    g.tensor.wait_ge(sem["ua%d" % late], _engines(T, topo, late))
+    f_late = layer1(late)
+    for s in order[1:-1]:
+        g.tensor.wait_ge(sem["arr%d" % s], _engines(T, topo, s))
+        f = layer1(s)
+        layer2(s, f, False, False)
+    g.tensor.wait_ge(sem["ub%d" % late], _engines(T, topo, late))
+    layer2(late, f_late, False, True)
 
     for p, (a, b) in enumerate(pieces):
         g.vector.wait_ge(sem["a%d" % p], n)
@@ -103,4 +139,4 @@ def rank_program(g, core, T, topo):
     g.sync.wait_ge(sem.cp, len(pieces))
     g.sync.dma_start(T.y[:, 0:W], T.ys[:, 0:W]).then_inc(sem.st, 16)
     g.sync.wait_ge(sem.st, 16)
-    g.wait_ge(sem.sent, _engines(T, topo, rank))
+    g.wait_ge(sem.sent, 3 * _engines(T, topo, rank))

@@ -30,15 +30,26 @@ SEMAPHORES = (["l1", "l2", "xl", "zs", "sent", "cp", "st"]
               + ["a%d" % p for p in range(NPIECE)])
 
 
-def _peers(T, rank):
+def _plan(T, j):
     n = len(T.cores)
-    return [T.cores[(rank + s) % n] for s in range(1, n)]
+    peers = [(j + s) % n for s in range(1, n)]
+    last = peers[-1]
+    items = [(last, "1")]
+    for p in peers[:-1]:
+        if p == peers[-2] and T.tables["WID"][p] > PIECE:
+            items += [(p, "1"), (p, "2")]
+        else:
+            items.append((p, "w"))
+    items.append((last, "2"))
+    return items
 
 
 def _mask(T, topo, rank):
     src = T.cores[rank]
     m = None
-    for p in _peers(T, rank):
+    for p in T.cores:
+        if p == src:
+            continue
         assert topo.may_write(src, p)
         m = topo.mask(src, p) if m is None else (m & topo.mask(src, p))
     return m
@@ -46,14 +57,6 @@ def _mask(T, topo, rank):
 
 def _engines(T, topo, rank):
     return bin(_mask(T, topo, rank)).count("1")
-
-
-def _ids(topo, dsts):
-    out = []
-    for p in dsts:
-        rid, pid, _se = topo.addr(p)
-        out.append(DstId(rid=rid, pnc=pid))
-    return out
 
 
 def rank_program(g, core, T, topo):
@@ -64,37 +67,31 @@ def rank_program(g, core, T, topo):
     W = T.tables["WID"][rank]
     sem = T.sem
     base = rank * SLOT
-    own1 = T.wall[:, base:base + D]
-    own2 = T.wall[:, base + D:base + SLOT]
-    own = T.wall[:, base:base + SLOT]
+    part = {"1": T.wall[:, base:base + D], "2": T.wall[:, base + D:base + SLOT], "w": T.wall[:, base:base + SLOT]}
+    name = {"1": "ua%d", "2": "ub%d", "w": "arr%d"}
 
-    g.sync.dma_start(own1, T.w1[:, :]).then_inc(sem.l1, 16)
-    g.sync.dma_start(own2, T.w2[:, :]).then_inc(sem.l2, 16)
-    g.scalar.wait_ge(sem.l1, 16)
+    g.sync.dma_start(part["1"], T.w1[:, :]).then_inc(sem.l1, 16)
+    g.sync.dma_start(part["2"], T.w2[:, :]).then_inc(sem.l2, 16)
+    if W <= PIECE:
+        g.scalar.wait_ge(sem.l1, 16)
     g.scalar.dma_start(T.xs[:, 0:W], T.x[:, 0:W]).then_inc(sem.xl, 16)
     g.vector.memset(T.zero[:, :], 0.0).then_inc(sem.zs, 1)
 
-    peers = _peers(T, rank)
-    whole, split = peers[:-1], peers[-1:]
     mask = _mask(T, topo, rank)
+    plan = _plan(T, rank)
     g.wait_ge(sem.l1, 16)
-    g.remote_dma_fused(
-        [RemoteDMATransfer(dst_ids=_ids(topo, split), dma_engine_mask=mask, remote_sem=sem["ua%d" % rank],
-                           srcs=[own1], dsts=[own1 for _p in split], alu_op=0)],
-        local_sem=sem.sent)
-    g.wait_ge(sem.l2, 16)
-    g.remote_dma_fused(
-        [RemoteDMATransfer(dst_ids=_ids(topo, whole), dma_engine_mask=mask, remote_sem=sem["arr%d" % rank],
-                           srcs=[own], dsts=[own for _p in whole], alu_op=0)],
-        local_sem=sem.sent)
-    g.remote_dma_fused(
-        [RemoteDMATransfer(dst_ids=_ids(topo, split), dma_engine_mask=mask, remote_sem=sem["ub%d" % rank],
-                           srcs=[own2], dsts=[own2 for _p in split], alu_op=0)],
-        local_sem=sem.sent)
+    have2 = False
+    for (p, what) in plan:
+        if what != "1" and not have2:
+            g.wait_ge(sem.l2, 16)
+            have2 = True
+        rid, pid, _se = topo.addr(T.cores[p])
+        g.remote_dma_fused(
+            [RemoteDMATransfer(dst_ids=[DstId(rid=rid, pnc=pid)], dma_engine_mask=mask,
+                               remote_sem=sem[name[what] % rank], srcs=[part[what]], dsts=[part[what]], alu_op=0)],
+            local_sem=sem.sent)
 
     pieces = [(a, min(a + PIECE, W)) for a in range(0, W, PIECE)]
-    order = [(rank - si) % n for si in range(n)]
-    late = order[-1]
     kk = [0]
 
     def layer1(s):
@@ -119,19 +116,46 @@ def rank_program(g, core, T, topo):
                             T.hs[:, s * TK + a:s * TK + b], start, stop).then_inc(sem["a%d" % p], 1)
 
     g.vector.wait_ge(sem.zs, 1)
-    g.tensor.wait_ge(sem.l1, 16)
-    g.tensor.wait_ge(sem.xl, 16)
-    f_own = layer1(rank)
-    g.tensor.wait_ge(sem.l2, 16)
-    layer2(rank, f_own, True, False)
-    g.tensor.wait_ge(sem["ua%d" % late], _engines(T, topo, late))
-    f_late = layer1(late)
-    for s in order[1:-1]:
-        g.tensor.wait_ge(sem["arr%d" % s], _engines(T, topo, s))
-        f = layer1(s)
-        layer2(s, f, False, False)
-    g.tensor.wait_ge(sem["ub%d" % late], _engines(T, topo, late))
-    layer2(late, f_late, False, True)
+
+    events = []
+    for s in range(n):
+        if s == rank:
+            continue
+        t = 0
+        for (p, what) in _plan(T, s):
+            t += 2 if what == "w" else 1
+            if p == rank:
+                events.append((t, s, what))
+    events.sort()
+    ops = [("1", rank, [(sem.l1, 16), (sem.xl, 16)]), ("2", rank, [(sem.l2, 16)])]
+    for (_t, s, what) in events:
+        w = [(sem[name[what] % s], _engines(T, topo, s))]
+        if what != "2":
+            ops.append(("1", s, w))
+            w = []
+        if what != "1":
+            ops.append(("2", s, w))
+    order, held = [], None
+    for op in ops:
+        if op[0] == "2":
+            if held is not None:
+                order.append(held)
+            held = op
+        else:
+            order.append(op)
+            if held is not None:
+                order.append(held)
+                held = None
+    order.append(held)
+    firsts = {}
+    seconds = [op for op in order if op[0] == "2"]
+    for op in order:
+        for (sm, v) in op[2]:
+            g.tensor.wait_ge(sm, v)
+        if op[0] == "1":
+            firsts[op[1]] = layer1(op[1])
+        else:
+            layer2(op[1], firsts[op[1]], op is seconds[0], op is seconds[-1])
 
     for p, (a, b) in enumerate(pieces):
         g.vector.wait_ge(sem["a%d" % p], n)
@@ -139,4 +163,4 @@ def rank_program(g, core, T, topo):
     g.sync.wait_ge(sem.cp, len(pieces))
     g.sync.dma_start(T.y[:, 0:W], T.ys[:, 0:W]).then_inc(sem.st, 16)
     g.sync.wait_ge(sem.st, 16)
-    g.wait_ge(sem.sent, 3 * _engines(T, topo, rank))
+    g.wait_ge(sem.sent, len(plan) * _engines(T, topo, rank))

from concourse.bass import DstId, RemoteDMATransfer
from concourse.mybir import AluOpType

N = 5
D = 128
TK = 256
PIECE = 128
NPIECE = TK // PIECE
NH = 6
SLOT = 2 * D

SCRATCH = {
    "wall": ("sbuf", [128, N * SLOT], "bfloat16"),
    "xs": ("sbuf", [128, TK], "bfloat16"),
    "zero": ("sbuf", [128, PIECE], "float32"),
    "hs": ("sbuf", [128, N * TK], "bfloat16"),
    "ys": ("sbuf", [128, TK], "bfloat16"),
}
for _i in range(NH):
    SCRATCH["h%d" % _i] = ("psum", [128, 512], "float32")
for _i in range(NPIECE):
    SCRATCH["y%d" % _i] = ("psum", [128, 512], "float32")

SEMAPHORES = (["l1", "l2", "xl", "zs", "sent", "cp", "st"]
              + ["ua%d" % j for j in range(N)]
              + ["ub%d" % j for j in range(N)]
              + ["arr%d" % j for j in range(N)]
              + ["m%d" % k for k in range(N * NPIECE)]
              + ["r%d" % k for k in range(N * NPIECE)]
              + ["a%d" % p for p in range(NPIECE)])


def _plan(T, j):
    n = len(T.cores)
    peers = [(j + s) % n for s in range(1, n)]
    last = peers[-1]
    items = [(last, "1")]
    for p in peers[:-1]:
        if p == peers[-2] and T.tables["WID"][p] > PIECE:
            items += [(p, "1"), (p, "2")]
        else:
            items.append((p, "w"))
    items.append((last, "2"))
    return items


def _mask(T, topo, rank):
    src = T.cores[rank]
    m = None
    for p in T.cores:
        if p == src:
            continue
        assert topo.may_write(src, p)
        m = topo.mask(src, p) if m is None else (m & topo.mask(src, p))
    return m


def _engines(T, topo, rank):
    return bin(_mask(T, topo, rank)).count("1")


def rank_program(g, core, T, topo):
    rank = T.rank_of(core)
    if rank is None:
        return
    n = len(T.cores)
    W = T.tables["WID"][rank]
    sem = T.sem
    base = rank * SLOT
    part = {"1": T.wall[:, base:base + D], "2": T.wall[:, base + D:base + SLOT], "w": T.wall[:, base:base + SLOT]}
    name = {"1": "ua%d", "2": "ub%d", "w": "arr%d"}

    g.sync.dma_start(part["1"], T.w1[:, :]).then_inc(sem.l1, 16)
    g.sync.dma_start(part["2"], T.w2[:, :]).then_inc(sem.l2, 16)
    if W <= PIECE:
        g.scalar.wait_ge(sem.l1, 16)
    g.scalar.dma_start(T.xs[:, 0:W], T.x[:, 0:W]).then_inc(sem.xl, 16)
    g.vector.memset(T.zero[:, :], 0.0).then_inc(sem.zs, 1)

    mask = _mask(T, topo, rank)
    plan = _plan(T, rank)
    g.wait_ge(sem.l1, 16)
    have2 = False
    for (p, what) in plan:
        if what != "1" and not have2:
            g.wait_ge(sem.l2, 16)
            have2 = True
        rid, pid, _se = topo.addr(T.cores[p])
        g.remote_dma_fused(
            [RemoteDMATransfer(dst_ids=[DstId(rid=rid, pnc=pid)], dma_engine_mask=mask,
                               remote_sem=sem[name[what] % rank], srcs=[part[what]], dsts=[part[what]], alu_op=0)],
            local_sem=sem.sent)

    pieces = [(a, min(a + PIECE, W)) for a in range(0, W, PIECE)]
    kk = [0]

    def layer1(s):
        first = kk[0]
        for (a, b) in pieces:
            k = kk[0]
            if k >= NH:
                g.tensor.wait_ge(sem["r%d" % (k - NH)], 1)
            hb = T["h%d" % (k % NH)]
            g.tensor.matmul(hb[:, 0:b - a], T.wall[:, s * SLOT:s * SLOT + D], T.xs[:, a:b],
                            True, True).then_inc(sem["m%d" % k], 1)
            g.vector.wait_ge(sem["m%d" % k], 1)
            g.vector.tensor_tensor(T.hs[:, s * TK + a:s * TK + b], hb[:, 0:b - a], T.zero[:, 0:b - a],
                                   AluOpType.max).then_inc(sem["r%d" % k], 1)
            kk[0] += 1
        return first

    def layer2(s, first, start, stop):
        for p, (a, b) in enumerate(pieces):
            g.tensor.wait_ge(sem["r%d" % (first + p)], 1)
            g.tensor.matmul(T["y%d" % p][:, 0:b - a], T.wall[:, s * SLOT + D:(s + 1) * SLOT],
                            T.hs[:, s * TK + a:s * TK + b], start, stop).then_inc(sem["a%d" % p], 1)

    g.vector.wait_ge(sem.zs, 1)

    events = []
    for s in range(n):
        if s == rank:
            continue
        t = 0
        for (p, what) in _plan(T, s):
            t += 2 if what == "w" else 1
            if p == rank:
                events.append((t, s, what))
    events.sort()
    ops = [("1", rank, [(sem.l1, 16), (sem.xl, 16)]), ("2", rank, [(sem.l2, 16)])]
    for (_t, s, what) in events:
        w = [(sem[name[what] % s], _engines(T, topo, s))]
        if what != "2":
            ops.append(("1", s, w))
            w = []
        if what != "1":
            ops.append(("2", s, w))
    order, held = [], None
    for op in ops:
        if op[0] == "2":
            if held is not None:
                order.append(held)
            held = op
        else:
            order.append(op)
            if held is not None:
                order.append(held)
                held = None
    order.append(held)
    firsts = {}
    seconds = [op for op in order if op[0] == "2"]
    for op in order:
        for (sm, v) in op[2]:
            g.tensor.wait_ge(sm, v)
        if op[0] == "1":
            firsts[op[1]] = layer1(op[1])
        else:
            layer2(op[1], firsts[op[1]], op is seconds[0], op is seconds[-1])

    for p, (a, b) in enumerate(pieces):
        g.vector.wait_ge(sem["a%d" % p], n)
        g.vector.tensor_copy(T.ys[:, a:b], T["y%d" % p][:, 0:b - a]).then_inc(sem.cp, 1)
    g.sync.wait_ge(sem.cp, len(pieces))
    g.sync.dma_start(T.y[:, 0:W], T.ys[:, 0:W]).then_inc(sem.st, 16)
    g.sync.wait_ge(sem.st, 16)
    g.wait_ge(sem.sent, len(plan) * _engines(T, topo, rank))
